import numpy as np, ml_dtypes
CORES = [48,51,52,55]
N = 4
BF = ml_dtypes.bfloat16
def gentries(a):
    return np.ascontiguousarray(a.reshape(8, 16, -1).transpose(0, 2, 1)).reshape(8, -1)
def gtable(e):
    e = np.asarray(e); return np.ascontiguousarray(e.reshape(8, -1, 16).transpose(0, 2, 1)).reshape(128, -1).astype(np.int32)
def f(rng, *shape):
    return (rng.standard_normal(shape, dtype=np.float32) * np.exp2(rng.integers(-2, 3, shape[:-1] + (1,)))).astype(BF)
def wide(rng, *shape):
    v = f(rng, *shape).astype(np.float32); k = shape[:-2] + (1, shape[-1])
    return (v * np.exp2(rng.integers(-6, 7, k)) * (rng.random(k) > 0.0625)).astype(BF)
F, P, KD, GEN, LG, RO = 2048, 2048, 2, 8, 3, 3
S, H = F + 2 * P, F // 2
def pointers(pl, b):
    return np.concatenate([np.broadcast_to(np.arange(F), (N, 8, F)), 2 * pl + b], axis=2)
def rise(q):
    for i in range(LG): q = np.take_along_axis(q, q, 2)
    return q
def alleles(rng):
    u = rng.random((N, 8, 16, F), dtype=np.float32)
    return np.floor(16 * u * np.sqrt(u)) * np.exp2(rng.integers(-2, 3, (N, 8, 16, 1))).astype(np.float32)
def generations(rng):
    e = rng.choice(np.array([0.7, 1.0, 1.4]), (N, 8, 1))
    return np.minimum(1 + (GEN * rng.random((N, 8, P)) ** e).astype(np.int64), GEN)
def pedigree(rng, gl, near):
    pl = np.zeros((N, 8, 2 * P), np.int64)
    for r in range(N):
        for g in range(8):
            k = gl[r, g]; o = np.argsort(k, kind="stable"); ids = np.concatenate([np.arange(H), H + o])
            under = np.searchsorted(k[o], np.arange(GEN + 2)); kk = np.repeat(k, 2)
            top = H + under[kk]; low = np.where(kk == 1, 0, H + under[kk - 1])
            low = np.where((rng.random(2 * P) < near) & (low < top), low, 0)
            pl[r, g] = ids[low + (rng.random(2 * P) * (top - low)).astype(np.int64)]
    return pl
def kids(rng, pl):
    kl = rng.integers(F, S, (N, 8, KD, P))
    for r in range(N):
        for g in range(8):
            v = pl[r, g]; o = np.lexsort((rng.random(2 * P), v)); at = np.searchsorted(v[o], H + np.arange(P + 1))
            for k in range(KD):
                kl[r, g, k] = np.where(at[:-1] + k < at[1:], F + o[np.minimum(at[:-1] + k, 2 * P - 1)], kl[r, g, k])
    return kl
def phenotypes(rng, al, pl, tb):
    a = rise(pointers(pl, tb))[:, :, F:].reshape(N, 8, 1, P, 2)
    y = np.maximum(np.take_along_axis(al, a[..., 0], 3), np.take_along_axis(al, a[..., 1], 3))
    return np.where(rng.random(y.shape) < 0.0625, np.take_along_axis(al, rng.integers(0, F, y.shape), 3), y)
def start(rng, tb):
    return tb ^ (rng.random((1, 8, 2 * P)) < 0.2).astype(np.int64) ^ (rng.random((N, 8, 2 * P)) < 0.1).astype(np.int64)
def pack(al, y, pl, b, kl, gl):
    return {"fa": np.ascontiguousarray(al.reshape(N, 128, F)).astype(BF), "ph": np.ascontiguousarray(y.reshape(N, 128, P)).astype(BF),
            "par": np.stack([gtable(a) for a in pl]), "sw": np.stack([gtable(a) for a in b]),
            "kd": np.stack([gtable(a.reshape(8, -1)) for a in kl]), "gen": np.ascontiguousarray(gl).astype(np.int32)}
def finish(rng, al, gl, pl, kl):
    tb = rng.integers(0, 2, (N, 8, 2 * P)); y = phenotypes(rng, al, pl, tb)
    return pack(al, y, pl, start(rng, tb), kl, gl)
def own():
    return F + 2 * np.arange(P)[None, :] + np.arange(KD)[:, None] % 2
def setup_inputs(rng):
    al = alleles(rng); gl = generations(rng); pl = pedigree(rng, gl, 0.85)
    return finish(rng, al, gl, pl, kids(rng, pl))
def setup_inputs_deep(rng):
    al = alleles(rng); gl = np.tile(GEN - np.arange(P) * GEN // P, (N, 8, 1)); gl[:, 1::2] = rng.permuted(gl[:, 1::2], axis=2)
    pl = pedigree(rng, gl, 1.0); one = np.repeat(gl[:, 0], 2, axis=1) == 1
    pl[:, 0] = np.where(one, rng.choice(np.array([0, H - 1]), one.shape), pl[:, 0])
    return finish(rng, al, gl, pl, kids(rng, pl))
def setup_inputs_full(rng):
    h = H // 2; up = rng.integers(0, 2, (N, 8, H)); v = rng.integers(0, 4, (N, 8, 16, H, 2))
    tall = up[:, :, None, :h, None] == np.arange(2)
    v[:, :, :, :h] = np.where(tall, rng.integers(10, 16, (N, 8, 16, h, 2)), rng.integers(4, 10, (N, 8, 16, h, 2)))
    unit = np.exp2(rng.integers(-2, 3, (N, 8, 16, 1))).astype(np.float32); al = v.reshape(N, 8, 16, F).astype(np.float32) * unit
    e = rng.integers(0, 2, (8, P)); pl = rng.integers(h, H, (N, 8, P, 2)); tb = rng.integers(0, 2, (N, 8, P, 2)); b = tb.copy()
    gl = np.full((N, 8, P), 2); kl = rng.integers(F, S, (N, 8, KD, P)); near = np.zeros((8, P), bool); weak = np.zeros((N, 8, P), bool)
    top = min(GEN, 8); n = -(-P // (2 ** top - 1)); size = [P - n * (2 ** (top - 1) - 1)] + [n * 2 ** (top - i) for i in range(2, top + 1)]
    for g in range(8):
        o = rng.permutation(P); band = np.split(o, np.add.accumulate(size)[:-1]); hit = o
        if g % 2 == 0:
            hit = band[0][:size[0] // 2]; rest = band[0][size[0] // 2:]; near[g, hit] = rng.random(len(hit)) < 0.5
            for i in range(top): gl[:, g, band[i]] = i + 1
        for r in range(N):
            x = rng.integers(0, h, len(hit)); pl[r, g, hit, e[g, hit]] = x; tb[r, g, hit, e[g, hit]] = up[r, g, x]; b[r, g, hit, e[g, hit]] = 1 - up[r, g, x]
            if g % 2: continue
            kid = band[1]; s = e[g, kid]
            x = rng.permutation(np.concatenate([hit, rng.choice(hit, len(kid) - len(hit))])); z = rng.permutation(np.concatenate([rest, rng.choice(rest, len(kid) - len(rest))]))
            pl[r, g, kid, s] = H + x; tb[r, g, kid, s] = e[g, x]; b[r, g, kid, s] = e[g, x]; pl[r, g, kid, 1 - s] = H + z; weak[r, g, kid] = near[g, x]
            for i in range(2, top): pl[r, g, band[i]] = H + rng.permutation(band[i - 1]).reshape(-1, 2)
            w = pl[r, g].reshape(-1); far = np.flatnonzero(w >= H); one = F + 2 * np.arange(P); one[w[far] - H] = F + far; kl[r, g] = one
    pl = pl.reshape(N, 8, 2 * P); tb = tb.reshape(N, 8, 2 * P); b = b.reshape(N, 8, 2 * P)
    def seen(c):
        a = rise(pointers(pl, c))[:, :, F:].reshape(N, 8, 1, P, 2)
        return np.maximum(np.take_along_axis(al, a[..., 0], 3), np.take_along_axis(al, a[..., 1], 3))
    y = np.where(near[None, :, None, :], seen(b), seen(tb))
    off = weak[:, :, None, :] & (np.argsort(rng.random((N, 8, 16, P)), axis=2) >= 16 // (KD - 1))
    return pack(al, np.where(off, 16 * unit, y), pl, b, kl, gl)
def setup_inputs_ties(rng):
    al = alleles(rng); al[..., 1:H // 2:2] = al[..., 0:H // 2:2]
    lot = np.argsort(rng.random((8, P)), axis=1); mz = lot < P // 8; mx = lot < 5 * P // 8
    gl = generations(rng); gl[:, mz] = 2
    pl = pedigree(rng, gl, 0.85); v = pl.reshape(N, 8, P, 2)
    v[..., 0] = np.where(mz, rng.integers(0, H // 4, (N, 8, P)), v[..., 0]); v[..., 1] = np.where(mx, v[..., 0], v[..., 1])
    kl = np.where(mx[:, None, :], own(), kids(rng, pl))
    tb = rng.integers(0, 2, (N, 8, 2 * P)); w = tb.reshape(N, 8, P, 2)
    w[..., 0] = np.where(mx, 0, w[..., 0]); w[..., 1] = np.where(mx, 1, w[..., 1])
    y = phenotypes(rng, al, pl, tb); b = np.ascontiguousarray(start(rng, tb)); w = b.reshape(N, 8, P, 2)
    w[..., 1] = np.where(mx, w[..., 0], w[..., 1])
    return pack(al, y, pl, b, kl, gl)
def setup_inputs_kids(rng):
    al = alleles(rng); gl = generations(rng); gl[:, 3] = 2; gl[:, 3, 0] = 1; gl[:, 3, P - 1] = 1; gl[:, 7] = 1
    pl = pedigree(rng, gl, 0.85); two = np.repeat(gl[:, 3], 2, axis=1) == 2; one = np.repeat(gl[:, 5], 2, axis=1) == 1
    pl[:, 3] = np.where(two, rng.choice(np.array([H, H + P - 1]), two.shape), pl[:, 3])
    pl[:, 5] = np.where(one, rng.choice(np.array([0, H - 1]), one.shape), pl[:, 5])
    kl = kids(rng, pl); kl[:, 0::2] = kl[:, 0::2, :1].copy()
    kl[:, 1] = np.where(rng.random((N, KD, P)) < 0.5, own(), rng.choice(np.array([F, S - 1]), (N, KD, P)))
    return finish(rng, al, gl, pl, kl)
def setup_inputs_spread(rng):
    al = wide(rng, N, 128, F).astype(np.float32).reshape(N, 8, 16, F) * np.exp2(rng.integers(-40, 41, (N, 8, 16, 1))).astype(np.float32)
    gl = generations(rng); pl = pedigree(rng, gl, 0.6)
    return finish(rng, al, gl, pl, kids(rng, pl))
def check_inputs(d):
    bad = []
    for k in ("fa", "ph"):
        if not np.all(np.isfinite(d[k].astype(np.float32))): bad.append("finite numbers in " + k)
    low = len(bad)
    for k, lo, hi in (("par", 0, S // 2 - 1), ("sw", 0, 1), ("kd", F, S - 1), ("gen", 1, GEN)):
        if np.min(d[k]) < lo or np.max(d[k]) > hi: bad.append("range of " + k)
    if len(bad) == low:
        gl = d["gen"].astype(np.int64); pl = np.stack([gentries(a) for a in d["par"]]).astype(np.int64)
        age = np.concatenate([np.zeros((N, 8, H), np.int64), gl], axis=2)
        if np.any(np.take_along_axis(age, pl, 2) >= np.repeat(gl, 2, axis=2)): bad.append("generations of parents")
    return bad
def reference(fa, ph, par, sw, kd, gen):
    al = fa.astype(np.float32).reshape(N, 8, 16, F); y = np.repeat(ph.astype(np.float32).reshape(N, 8, 16, P), 2, axis=3)
    pl = np.stack([gentries(a) for a in par]).astype(np.int64); b = np.stack([gentries(a) for a in sw]).astype(np.int64)
    kl = np.stack([gentries(a) for a in kd]).astype(np.int64).reshape(N, 8, KD, P); gl = np.repeat(gen.astype(np.int64), 2, axis=2)
    first = np.broadcast_to(np.arange(F), (N, 8, F)); slot = np.arange(F, S).reshape(P, 2); even = np.arange(2 * P) % 2 == 0
    def match(a, other):
        u = np.take_along_axis(al, a[:, :, None, :], 3); v = np.take_along_axis(al, other[:, :, None, :], 3)
        return np.add.reduce(y == np.maximum(u, v), axis=2, dtype=np.int64)
    for t in range(1, RO + 1):
        q = pointers(pl, b); a = rise(q)
        alt = np.concatenate([first, np.take_along_axis(a, q[:, :, F:] ^ 1, 2)], axis=2)
        alt2 = np.take_along_axis(alt, q[:, :, F:], 2)
        mine = a[:, :, F:]; other = np.ascontiguousarray(mine.reshape(N, 8, P, 2)[..., ::-1]).reshape(N, 8, 2 * P)
        base = match(mine, other)
        g0 = match(alt[:, :, F:], other) - base; g1 = match(alt2, other) - base
        vote = g0.reshape(N, 8, P, 2)
        for k in range(KD):
            up = np.take_along_axis(q, kl[:, :, k], 2); gk = np.take_along_axis(g1, kl[:, :, k] - F, 2)
            vote = vote + np.where(up[..., None] == slot, gk[..., None], 0)
        vote = np.add.reduce(vote, axis=0)
        mate = np.ascontiguousarray(vote[..., ::-1]).reshape(8, 2 * P); vote = vote.reshape(8, 2 * P)
        go = (vote > 0) & ((vote > mate) | ((vote == mate) & even))
        b = np.where(go[None] & (gl % 2 == t % 2), 1 - b, b)
    a = rise(pointers(pl, b))[:, :, F:]
    return {"ya": np.stack([gtable(e) for e in a]).astype(np.float32), "ys": np.stack([gtable(e) for e in b]).astype(np.float32)}

from concourse.bass import DstId, RemoteDMATransfer
from concourse.mybir import AluOpType as A, ActivationFunctionType as AF

F = 2048
S = 6144
RO = 3
BF, F32, I32, U16 = "bfloat16", "float32", "int32", "uint16"
NSEND = 2 * RO + 1

SCRATCH = {
    "tq": ("sbuf", [128, S], BF), "b1": ("sbuf", [128, S], BF), "xa": ("sbuf", [128, S], BF), "xb": ("sbuf", [128, S], BF),
    "yy": ("sbuf", [128, 2048], BF), "vv": ("sbuf", [128, 4096], BF), "ww": ("sbuf", [128, 4096], BF),
    "ev": ("sbuf", [128, 4096], BF), "ew": ("sbuf", [128, 4096], BF), "eb": ("sbuf", [128, 2048], BF),
    "ko": ("sbuf", [128, 4096], BF), "grow": ("sbuf", [128, 2048], BF),
    "pari": ("sbuf", [128, 256], I32), "swi": ("sbuf", [128, 256], I32), "kdi": ("sbuf", [128, 256], I32),
    "geni": ("sbuf", [128, 128], I32), "genb": ("sbuf", [128, 128], BF),
    "t0": ("sbuf", [128, 256], I32), "t1": ("sbuf", [128, 256], I32), "t2": ("sbuf", [128, 256], I32),
    "t3": ("sbuf", [128, 256], I32),
    "nh": ("sbuf", [128, 256], BF), "lo": ("sbuf", [128, 256], BF),
    "ph1": ("sbuf", [128, 256], BF), "ph2": ("sbuf", [128, 256], BF),
    "k1": ("sbuf", [128, 256], BF), "k2": ("sbuf", [128, 256], BF), "k3": ("sbuf", [128, 256], BF),
    "kf": ("sbuf", [128, 256], F32), "vt": ("sbuf", [128, 256], F32), "vti": ("sbuf", [128, 256], F32),
    "swb": ("sbuf", [128, 1024], BF), "pen": ("sbuf", [128, 512], BF), "thr": ("sbuf", [128, 256], F32),
    "hh": ("sbuf", [128, 512], BF), "vote": ("sbuf", [128, 768], BF), "land": ("sbuf", [128, 1024 * NSEND], BF),
    "lp": ("sbuf", [128, 256], U16), "l2": ("sbuf", [128, 256], U16), "l4": ("sbuf", [128, 256], U16),
    "lv": ("sbuf", [128, 256], U16), "lr": ("sbuf", [128, 256], U16), "lk0": ("sbuf", [128, 256], U16),
    "lk": ("sbuf", [128, 256], U16),
    "vu": ("sbuf", [128, 512], F32), "vui": ("sbuf", [128, 512], F32), "km": ("sbuf", [128, 512], F32),
    "kx": ("sbuf", [128, 512], BF), "col3": ("sbuf", [128, 8], F32),
    "oa": ("sbuf", [128, 256], F32), "osw": ("sbuf", [128, 256], F32),
    "pi": ("sbuf", [128, 128], I32), "pj": ("sbuf", [128, 128], I32), "pk": ("sbuf", [128, 8], I32),
    "it": ("sbuf", [128, 128], BF), "it128": ("sbuf", [128, 128], BF), "ct": ("sbuf", [128, 128], BF),
    "ct16": ("sbuf", [128, 128], BF), "cols": ("sbuf", [128, 8], F32), "col2": ("sbuf", [128, 8], F32),
    "one": ("sbuf", [128, 144], BF), "blk": ("sbuf", [128, 144], BF), "ws": ("sbuf", [128, 144], BF),
    "wc": ("sbuf", [128, 144], BF), "wp": ("sbuf", [128, 144], BF), "wr": ("sbuf", [128, 144], BF),
    "wk": ("sbuf", [128, 144], BF), "wb": ("sbuf", [128, 144], BF), "wb0": ("sbuf", [128, 144], BF),
    "wg": ("sbuf", [128, 144], BF), "wq": ("sbuf", [128, 144], BF),
    "eye": ("sbuf", [128, 128], BF), "eye128": ("sbuf", [128, 128], BF), "eyen": ("sbuf", [128, 128], BF),
    "eye16": ("sbuf", [128, 128], BF), "eyem": ("sbuf", [128, 128], BF), "swp": ("sbuf", [128, 128], BF),
}
BANKS = ["cv0", "cv1", "mx0", "mx1", "mx2", "mx3", "vt0", "vt1"]
for _b in BANKS:
    SCRATCH[_b] = ("psum", [128, 512], F32)

NDMA = 64
SEMAPHORES = ["qv", "qa", "qp", "qg", "sent"] + ["arr%d" % i for i in range(NSEND)] + ["dm%d" % i for i in range(NDMA)]
GC = 25
NV = 16


def rank_program(g, core, T, topo):
    rank = T.rank_of(core)
    if rank is None:
        return
    Q = {"v": g.vector, "a": g.scalar, "p": g.tensor, "g": g, "s": g.sync}
    ops = []

    def R(name, lo, hi, step=1, row=None, np_=128):
        if row is not None:
            ap = T[name][row:128:16, lo:hi]
        elif step != 1:
            ap = T[name][0:np_, lo:hi:step]
        else:
            ap = T[name][0:np_, lo:hi]
        return (ap, (name, lo, hi, row))

    def op(q, fn, reads, writes, kind="c", sem=None):
        ops.append({"q": q, "fn": fn, "r": [x[1] for x in reads], "w": [x[1] for x in writes], "k": kind, "sem": sem})

    def dma(q, out, in_):
        rd = [in_] if in_[1] else []
        wr = [out] if out[1] else []
        op(q, lambda: Q[q].dma_start(out[0], in_[0]), rd, wr, "d")

    def ext(ap):
        return (ap, None)

    def copy(out, in_):
        op("v", lambda: g.vector.tensor_copy(out[0], in_[0]), [in_], [out])

    def ts(out, in_, s1, o0, s2=None, o1=None):
        if o1 is None:
            op("v", lambda: g.vector.tensor_scalar(out[0], in_[0], s1, None, o0), [in_], [out])
        else:
            op("v", lambda: g.vector.tensor_scalar(out[0], in_[0], s1, s2, o0, o1), [in_], [out])

    def tt(out, a, b, o):
        op("v", lambda: g.vector.tensor_tensor(out[0], a[0], b[0], o), [a, b], [out])

    def act(out, in_, func, bias=0.0, scale=1.0):
        if isinstance(bias, tuple):
            op("a", lambda: g.scalar.activation(out[0], in_[0], func, bias=bias[0], scale=scale), [in_, bias], [out])
        elif bias == 0.0:
            op("a", lambda: g.scalar.activation(out[0], in_[0], func, scale=scale), [in_], [out])
        else:
            op("a", lambda: g.scalar.activation(out[0], in_[0], func, bias=bias, scale=scale), [in_], [out])

    def iota(out, pat, base, cm, flag=True):
        if flag:
            op("g", lambda: g.iota(out[0], pat, base, cm, allow_small_or_imprecise_dtypes=True), [], [out])
        else:
            op("g", lambda: g.iota(out[0], pat, base, cm), [], [out])

    def sel(out, in_, pat, cmp, fill, base, cm):
        op("g", lambda: g.affine_select(out[0], in_[0], pat, cmp, fill, base, cm), [in_], [out])

    def part(out, terms, first, last):
        n = len(terms)
        for i, (l, r) in enumerate(terms):
            op("p", lambda l=l, r=r, i=i: g.tensor.matmul(out[0], l[0], r[0], first and i == 0, last and i == n - 1),
               [l, r], [out])

    def group(out, terms):
        part(out, terms, True, True)

    def gather(q, win, lst, c0, c1, out, o0):
        if c1 <= c0:
            return
        w = R(win, 0, S)
        l = R(lst, c0, c1)
        o = R(out, o0 + 16 * c0, o0 + 16 * c1)
        if q == "a":
            op("a", lambda: g.scalar.activation(o[0], w[0].indirect(l[0]), AF.Copy), [w, l], [o])
        else:
            op("v", lambda: g.vector.tensor_copy(o[0], w[0].indirect(l[0])), [w, l], [o])

    def both(win, lst, c0, c1, out, o0, extra=0):
        n = c1 - c0
        nv = max(0, min(n, int((n * GC - extra) / (2 * GC) / 2 + 0.5) * 2))
        gather("a", win, lst, c0, c1 - nv, out, o0)
        gather("v", win, lst, c1 - nv, c1, out, o0)

    def t_row(w, src, base, c0, c1):
        return [(R(w, 16 - i, 144 - i), R(src, base + 16 * c0 + i, base + 16 * c1, 16)) for i in range(16)]

    def t_slot(src, c0, c1):
        return [(R("ws", 16 - i, 144 - i), R(src, 2048 * (i % 2) + 8 * c0 + i // 2, 2048 * (i % 2) + 8 * c1, 8))
                for i in list(range(0, 16, 2)) + list(range(1, 16, 2))]

    def t_person(w, src, base, c0, c1, np_=128):
        return [(R(w, 16 - 2 * a, 144 - 2 * a, np_=np_), R(src, base + 8 * c0 + a, base + 8 * c1, 8, np_=np_))
                for a in range(8)]

    def to_row(q, row, src, c0, h):
        dma(q, R("tq", F + 2048 * h, F + 2048 * h + 2048, row=row), R(src, c0, c0 + 128))

    eye = R("eye", 0, 128)

    def ptr_list(t, h, bank):
        c = 128 * h
        o = R(bank, 0, 128)
        e16 = R("eye16", 0, 128)
        group(o, [(e16, R("lo", c, c + 128)), (e16, R("nh", c, c + 128)), (eye, R("ph1", c, c + 128)),
                  (eye, R("ph2", c, c + 128)), (R("eyem", 0, 128), R("ph2", c, c + 128)),
                  (R("eye128", 0, 128), R("swb", 256 * t + c, 256 * t + c + 128))])
        copy(R("lp", c, c + 128), o)

    def alt_list(t, bank):
        o = R(bank, 0, 256)
        group(o, [(eye, R("nh", 0, 256)), (eye, R("lo", 0, 256)), (R("eyen", 0, 128), R("swb", 256 * t, 256 * t + 256))])
        ts(R("lv", 0, 256), o, 1.0, A.add)

    dma("s", R("pari", 0, 256), ext(T.par[:]))
    dma("a", R("swi", 0, 256), ext(T.sw[:]))
    dma("s", R("kdi", 0, 256), ext(T.kd[:]))
    dma("a", R("geni", 0, 128), ext(T.gen[:]))
    iota(R("pi", 0, 128), [[0, 128]], 0, 1, False)
    iota(R("ct16", 0, 128), [[16, 128]], 0, 0)
    iota(R("one", 0, 144), [[0, 144]], 1, 0)
    sel(eye, R("one", 0, 128), [[-1, 128]], A.is_equal, 0.0, 0, 1)
    op("v", lambda: g.vector.memset(T.tq[:, 0:F], 0.0), [], [R("tq", 0, F)])
    act(R("tq", 2 * F, S), R("tq", 0, F), AF.Identity, bias=1.0)
    op("v", lambda: g.vector.memset(T.tq[:, F:2 * F], 1.0), [], [R("tq", F, 2 * F)])
    ts(R("pj", 0, 128), R("pi", 0, 128), 15, A.bitwise_and)
    copy(R("it", 0, 128), R("pj", 0, 128))
    par = R("pari", 0, 256)
    t0, t1, t2, t3 = R("t0", 0, 256), R("t1", 0, 256), R("t2", 0, 256), R("t3", 0, 256)
    ts(t0, par, 63, A.bitwise_and)
    ts(t1, par, 4032, A.bitwise_and)
    dma("s", R("tq", 0, F, row=0), R("ct16", 0, 128))
    dma("a", R("tq", 0, F, row=1), R("it", 0, 128))
    ts(R("lo", 0, 256), t0, 2.0, A.mult)
    to_row("s", 1, "lo", 0, 0)
    to_row("a", 1, "lo", 128, 1)
    act(R("eye16", 0, 128), eye, AF.Copy, scale=1.0 / 16)
    ts(R("nh", 0, 256), t1, 2.0, A.mult)
    to_row("s", 0, "nh", 0, 0)
    to_row("a", 0, "nh", 128, 1)
    act(R("eyem", 0, 128), eye, AF.Copy, scale=-1.0 / 2048)
    copy(R("swb", 0, 256), R("swi", 0, 256))
    to_row("s", 2, "swb", 0, 0)
    to_row("a", 2, "swb", 128, 1)
    act(R("eye128", 0, 128), eye, AF.Copy, scale=128.0)
    ts(t2, par, 3072, A.bitwise_and)
    ts(t3, par, 7, A.bitwise_and)
    ts(R("ph1", 0, 256), t2, 1.875, A.mult)
    ts(R("ph2", 0, 256), t3, 256.0, A.mult)
    ptr_list(0, 0, "mx2")
    ptr_list(0, 1, "mx3")
    iota(R("ct", 0, 128), [[1, 128]], 0, 0)
    iota(R("b1", 0, F), [[0, F]], 0, 0)
    w144 = lambda n: R(n, 0, 144)
    sel(w144("blk"), w144("one"), [[-16, 9], [0, 16]], A.is_ge, 0.0, 16, 1)
    sel(w144("blk"), w144("blk"), [[16, 9], [0, 16]], A.is_ge, 0.0, -1, -1)
    sel(w144("ws"), w144("blk"), [[0, 9], [1, 16]], A.is_equal, 0.0, 0, 0)
    sel(w144("wc"), w144("ws"), [[16, 9], [0, 16]], A.is_ge, 0.0, -14, -1)
    act(R("it128", 0, 128), R("it", 0, 128), AF.Copy, scale=128.0)
    act(R("eyen", 0, 128), eye, AF.Copy, scale=-1.0)
    act(R("col2", 0, 1), R("it", 0, 1), AF.Copy, scale=2.0)
    dma("s", R("b1", 0, F, row=0), R("it128", 0, 128))
    dma("s", R("b1", 0, F, row=1), R("ct", 0, 128))
    dma("s", R("xa", 0, F), ext(T.fa[:]))
    dma("s", R("xb", 0, F), ext(T.fa[:]))
    dma("s", R("yy", 0, 2048), ext(T.ph[:]))
    sel(w144("wr"), w144("wc"), [[-16, 9], [1000, 16]], A.not_equal, -1.0, 14, 1)
    sel(w144("wr"), w144("wr"), [[-16, 9], [1000, 16]], A.not_equal, 1.0, 13, 1)
    sel(w144("wb0"), w144("blk"), [[0, 9], [-1, 16]], A.is_ge, 0.0, 1, 0)
    sel(R("wg", 0, 144, np_=8), R("one", 0, 144, np_=8), [[-1, 72], [0, 2]], A.is_equal, 0.0, 8, 8)
    iota(w144("wk"), [[0, 144]], 0, 0)
    sel(w144("wk"), w144("wk"), [[-16, 9], [1000, 16]], A.not_equal, 1.0, 12, 1)
    sel(w144("wk"), w144("wk"), [[-16, 9], [1000, 16]], A.not_equal, -1.0, 11, 1)
    sel(w144("wk"), w144("wk"), [[-16, 9], [1000, 16]], A.not_equal, 1.0, 11 - 1000, 1)
    sel(w144("wq"), w144("wb0"), [[16, 9], [0, 16]], A.is_ge, 0.0, -15, -1)
    iota(R("vui", 0, 256), [[0, 2], [16, 128]], 2047, 0)
    iota(R("vui", 256, 512), [[1024, 2], [0, 2], [16, 64]], 4095, 0)
    sel(R("swp", 0, 128), R("one", 0, 128), [[-2, 64], [1, 2]], A.is_equal, 0.0, -1, 1)
    sel(w144("wp"), w144("ws"), [[16, 9], [0, 16]], A.is_ge, 0.0, -15, -1)
    iota(R("vti", 0, 256), [[0, 2], [32, 128]], 2048, 0)

    def kid_labels():
        kd = R("kdi", 0, 256)
        ts(R("k1", 0, 256), kd, 4096.0, A.is_ge, 2048.0, A.mult)
        ts(t0, kd, 15, A.bitwise_and)
        ts(t1, kd, 4, A.logical_shift_right, 127, A.bitwise_and)
        copy(R("k2", 0, 256), t0)
        copy(R("k3", 0, 256), t1)
        group(R("mx0", 0, 256), [(eye, R("k1", 0, 256)), (R("eye128", 0, 128), R("k2", 0, 256)), (eye, R("k3", 0, 256))])

    def parity_rows():
        ts(R("pj", 0, 128), R("geni", 0, 128), 1, A.bitwise_and)
        ts(R("pk", 0, 1), R("pi", 0, 1), 1, A.bitwise_and)
        copy(R("genb", 0, 128), R("pj", 0, 128))
        ts(R("cols", 0, 1), R("pk", 0, 1), -1.0, A.add)
        tt(R("col3", 0, 1), R("it", 0, 1), R("cols", 0, 1), A.subtract)
        dma("s", R("grow", 0, 2048, np_=8), R("genb", 0, 128))

    others = [c for c in T.cores if c != core]
    mask = topo.mask(core, others[0])
    for c in others[1:]:
        mask &= topo.mask(core, c)
    dst_ids = [DstId(rid=topo.addr(c)[0], pnc=topo.addr(c)[1]) for c in others]
    nsent = [0]
    width = bin(mask).count("1")

    def send(name, lo, hi):
        n = nsent[0]
        nsent[0] += 1
        src = R(name, lo, hi)
        at = 1024 * n + 256 * rank
        dst = T.land[:, at:at + hi - lo]
        tr = RemoteDMATransfer(dst_ids=dst_ids, dma_engine_mask=mask, remote_sem=T.sem["arr%d" % n],
                               srcs=[src[0]], dsts=[dst for _ in others])
        op("g", lambda: g.remote_dma_fused([tr], local_sem=T.sem.sent), [src], [], "r")
        op("x", None, [], [R("land", 1024 * n, 1024 * n + 1024)], "x", ("arr%d" % n, width * len(others)))
        own = [R(name, c, c + 128) for c in range(lo, hi, 128)]
        got = [R("land", 1024 * n + 256 * r + c, 1024 * n + 256 * r + c + 128)
               for r in range(len(T.cores)) if r != rank for c in range(0, hi - lo, 128)]
        return own, got

    def decide(t, h, bs, bz, sent):
        c = 128 * h
        early = [x for own, got in sent for x in own] + [x for own, got in sent[:-1] for x in got]
        late = sent[-1][1]
        s, z = R(bs, 0, 128), R(bz, 0, 128)
        swp = R("swp", 0, 128)
        pc = 256 * (t % 2) + c
        part(s, [(eye, x) for x in [R("pen", pc, pc + 128)] + early], True, False)
        group(z, [(swp, x) for x in early + late])
        part(s, [(eye, x) for x in late], False, True)
        th = R("thr", c, c + 128)
        act(th, z, AF.Relu, bias=R("cols", 0, 1))
        tt(s, s, th, A.is_gt)
        tt(R("swb", 256 * (t + 1) + c, 256 * (t + 1) + c + 128), s, R("swb", 256 * t + c, 256 * t + c + 128), A.not_equal)
        to_row("s", 2, "swb", 256 * (t + 1) + c, h)

    def climb(first):
        if first:
            kid_labels()
        both("tq", "lp", 0, 128, "b1", F, 1300 if first else 0)
        group(R("cv0", 0, 128), t_row("wc", "b1", F, 0, 128))
        if first:
            ts(R("lk0", 0, 256), R("mx0", 0, 256), 2048.0, A.add)
            parity_rows()
        both("tq", "lp", 128, 256, "b1", F, 1100 if first else 150)
        copy(R("l2", 0, 128), R("cv0", 0, 128))
        group(R("cv1", 0, 128), t_row("wc", "b1", F, 128, 256))
        if first:
            act(R("kf", 0, 256), R("mx0", 0, 256), AF.Identity, bias=2048.0)
        both("b1", "l2", 0, 128, "xa", F, 0 if first else 150)
        copy(R("l2", 128, 256), R("cv1", 0, 128))
        group(R("cv0", 0, 128), t_row("wc", "xa", F, 0, 128))
        both("b1", "l2", 128, 256, "xa", F, 150)
        copy(R("l4", 0, 128), R("cv0", 0, 128))
        group(R("cv1", 0, 128), t_row("wc", "xa", F, 128, 256))

    MX = ["mx0", "mx1", "mx2", "mx3"]

    def partner(n):
        n4 = n % 4
        for e in range(2):
            lo = F + 1024 * n4 + 1 - e
            group(R(MX[2 * (n % 2) + e], 0, 512), [(eye, R("xa", lo, F + 1024 * n4 + 1024, 2))])

    def matches(n, src, dst, early=None, between=None):
        n4 = n % 4
        for e in range(2):
            b = R(MX[2 * (n % 2) + e], 0, 512)
            tt(b, R(src, 1024 * n4 + e, 1024 * n4 + 1024, 2), b, A.max)
            if early and e == 0:
                early()
        if between:
            between()
        for e in range(2):
            b = R(MX[2 * (n % 2) + e], 0, 512)
            tt(R(dst, 2048 * e + 512 * n4, 2048 * e + 512 * n4 + 512), b, R("yy", 512 * n4, 512 * n4 + 512), A.is_equal)

    def base_fill(n):
        group(R(MX[n], 0, 512), [(eye, R("xa", F + 1024 * n + 1, F + 1024 * n + 1024, 2))])

    def base(n):
        for k in range(2):
            b = R(MX[n], 256 * k, 256 * k + 256)
            lo = F + 1024 * n + 512 * k
            tt(b, R("xa", lo, lo + 512, 2), b, A.max)
        for k in range(2):
            b = R(MX[n], 256 * k, 256 * k + 256)
            p = 512 * n + 256 * k
            tt(R("eb", p, p + 256), b, R("yy", p, p + 256), A.is_equal)

    def t_base(c0, c1):
        return t_person("wb", "eb", 0, c0, c1)

    def g1_conv(n):
        group(R("cv%d" % (n // 2), 64 * (n % 2), 64 * (n % 2) + 64),
              t_base(64 * n, 64 * n + 64) + t_slot("ew", 64 * n, 64 * n + 64))

    def kid_rows(t, h):
        c = 128 * h
        b = R("cv%d" % h, 0, 128)
        copy(R("hh", c, c + 128), b)
        to_row("s", 4, "hh", c, h)
        tt(R("hh", 256 + c, 256 + c + 128), b, R("swb", 256 * t + c, 256 * t + c + 128), A.mult)
        to_row("s", 5, "hh", 256 + c, h)

    def kids(lst, k, c0, c1, nv=0):
        gather("a", "tq", lst, 128 * k + c0 // 2, 128 * k + c1 // 2 - nv, "ko", 0)
        gather("v", "tq", lst, 128 * k + c1 // 2 - nv, 128 * k + c1 // 2, "ko", 0)

    def t_kid(k, c0, c1):
        return t_person("wk", "ko", 2048 * k, c0, c1)

    def kid_raw(k, c0, c1, b):
        n = c1 - c0
        o = 2 * (c0 % 128) + n * k
        group(R(b, o, o + n), t_person("wq", "ko", 2048 * k, c0, c1))
        group(R(b, 256 + o, 256 + o + n), t_kid(k, c0, c1))

    def kid_mask(c0, c1, b):
        n = 2 * (c1 - c0)
        o = 2 * (c0 % 128)
        m = R("km", 2 * c0, 2 * c0 + n)
        tt(m, R(b, o, o + n), R("vu", 2 * c0, 2 * c0 + n), A.is_equal)
        tt(R("kx", 2 * c0, 2 * c0 + n), R(b, 256 + o, 256 + o + n), m, A.mult)
        return [(eye, R("kx", 2 * c0 + k * n // 2, 2 * c0 + (k + 1) * n // 2)) for k in range(2)]

    def clean_kids(c, b):
        v = R(b, 0, 128)
        group(v, t_row("wp", "ko", 0, c, c + 128))
        tt(v, v, R("vt", c, c + 128), A.is_equal)
        tt(v, v, R("kf", c, c + 128), A.mult)
        copy(R("lk", c, c + 128), v)

    for t in range(RO):
        first = t == 0
        climb(first)
        both("xa", "l4", 0, 128, "xb", F, 300 if first else 150)
        copy(R("l4", 128, 256), R("cv1", 0, 128))
        if first:
            alt_list(0, "mx1")
            act(w144("wb"), w144("wb0"), AF.Copy, scale=-1.0)
        group(R("vt0", 0, 256), t_row("wr", "b1", F, 0, 256))
        both("xa", "l4", 128, 256, "xb", F, 150 if first else 0)
        gather("v", "xb", "l4", 0, 64, "xa", F)
        for n in range(1, 4):
            gather("a", "xb", "l4", 64 * n, 64 * n + 64, "xa", F)
        copy(R("lr", 0, 256), R("vt0", 0, 256))
        for n in range(4):
            base_fill(n)
        for n in range(4):
            gather("a", "xa", "lr", 64 * n, 64 * n + 64, "ww", 0)
        if first:
            group(R("cv1", 0, 256), t_person("wg", "grow", 0, 0, 256, np_=8))
            act(R("pen", 0, 256), R("cv1", 0, 256), AF.Identity, bias=-1024.0, scale=1024.0)
            act(R("pen", 256, 512), R("cv1", 0, 256), AF.Copy, scale=-1024.0)
        base(0)
        base(1)
        partner(0)
        base(2)
        base(3)
        partner(1)
        for n in range(4):
            gather("a", "xa", "lv", 64 * n, 64 * n + 64, "vv", 0)
        if first:
            act(R("vt", 0, 256), R("vti", 0, 256), AF.Identity, bias=R("col2", 0, 1))
            act(R("vu", 0, 512), R("vui", 0, 512), AF.Identity, bias=R("col3", 0, 1))
        va, v2, v3 = R("vt0", 0, 128), R("vt1", 0, 64), R("mx0", 0, 64) if first else R("cv0", 0, 64)
        part(va, t_base(0, 128), True, False)
        part(v2, t_base(128, 192), True, False)
        matches(0, "ww", "ew")
        partner(2)
        g1_conv(0)
        matches(1, "ww", "ew")
        partner(3)
        g1_conv(1)
        matches(2, "ww", "ew")
        kid_rows(t, 0)
        partner(4)
        g1_conv(2)
        if not first:
            part(v3, t_base(192, 256), True, False)
        matches(3, "ww", "ew")
        g1_conv(3)
        partner(5)
        matches(4, "vv", "ev", early=lambda: kid_rows(t, 1))
        if t + 1 == RO:
            for r in range(3):
                dma("s", R("xa", 0, F, row=r), R("b1", 0, F, row=r))
        partner(6)
        matches(5, "vv", "ev")
        partner(7)
        part(va, t_slot("ev", 0, 128), False, first)
        v0 = 256 * t
        vb = v0 + 128
        half = []
        if first:
            for k in range(2):
                kids("lk0", k, 0, 128)
                kid_raw(k, 0, 128, "cv0")
            act(R("vote", v0, vb), va, AF.Copy)
            half.append(send("vote", v0, vb))
            matches(6, "vv", "ev")
            part(v2, t_slot("ev", 128, 192), False, False)
            for k in range(2):
                kids("lk0", k, 128, 192)
            kid_raw(0, 128, 192, "cv1")
            matches(7, "vv", "ev", between=lambda: kid_mask(0, 128, "cv0"))
            half.append(send("kx", 0, 256))
            kid_raw(1, 128, 192, "cv1")
            part(v3, t_base(192, 256), True, False)
            kids("lk0", 0, 192, 256)
            kids("lk0", 1, 192, 256, NV)
            kid_raw(0, 192, 256, "mx1")
            part(v3, t_slot("ev", 192, 256), False, False)
            part(v2, kid_mask(128, 192, "cv1"), False, True)
            kid_raw(1, 192, 256, "mx1")
            act(R("vote", vb, vb + 64), v2, AF.Copy)
            part(v3, kid_mask(192, 256, "mx1"), False, True)
        else:
            for k in range(2):
                kids("lk", k, 0, 128)
                part(va, t_kid(k, 0, 128), False, k == 1)
            matches(6, "vv", "ev")
            part(v2, t_slot("ev", 128, 192), False, False)
            for k in range(2):
                kids("lk", k, 128, 192)
                part(v2, t_kid(k, 128, 192), False, k == 1)
            act(R("vote", v0, vb), va, AF.Copy)
            half.append(send("vote", v0, vb))
            matches(7, "vv", "ev")
            kids("lk", 0, 192, 256)
            act(R("vote", vb, vb + 64), v2, AF.Copy)
            kids("lk", 1, 192, 256, NV)
            part(v3, t_kid(0, 192, 256) + t_slot("ev", 192, 256) + t_kid(1, 192, 256), False, True)
        copy(R("vote", vb + 64, vb + 128), v3)
        last = [send("vote", vb, vb + 128)]
        decide(t, 0, "vt0", "cv1", half)
        ptr_list(t + 1, 0, "mx2")
        if first:
            clean_kids(0, "cv0")
        decide(t, 1, "mx0", "mx1", last)
        ptr_list(t + 1, 1, "mx3")
        if t + 1 < RO:
            alt_list(t + 1, "vt1")
        if first:
            clean_kids(128, "cv1")

    act(R("osw", 0, 256), R("swb", 256 * RO, 256 * RO + 256), AF.Copy)
    dma("s", ext(T.ys[:]), R("osw", 0, 256))
    climb(False)
    both("xa", "l4", 0, 128, "xb", F, 150)
    copy(R("l4", 128, 256), R("cv1", 0, 128))
    group(R("cv0", 0, 128), t_row("wc", "xb", F, 0, 128))
    both("xa", "l4", 128, 192, "xb", F, 0)
    group(R("cv1", 0, 64), t_row("wc", "xb", F, 128, 192))
    both("xa", "l4", 192, 256, "xb", F, 0)
    group(R("mx0", 0, 64), t_row("wc", "xb", F, 192, 256))
    copy(R("oa", 0, 128), R("cv0", 0, 128))
    dma("s", ext(T.ya[:, 0:128]), R("oa", 0, 128))
    act(R("oa", 128, 192), R("cv1", 0, 64), AF.Copy)
    copy(R("oa", 192, 256), R("mx0", 0, 64))
    dma("s", ext(T.ya[:, 128:256]), R("oa", 128, 256))

    emit(ops, Q, T, nsent[0] * width)


def emit(ops, Q, T, nsent):
    seen = {}
    clock = {q: {} for q in Q}
    count = {}
    for i, o in enumerate(ops):
        key = o["q"] if o["k"] in ("c", "r") else ("u", i)
        count[key] = count.get(key, 0) + 1
        o["key"], o["n"], o["sig"], o["waits"] = key, count[key], False, []
        need = {}
        for acc, wr in [(x, False) for x in o["r"]] + [(x, True) for x in o["w"]]:
            name, lo, hi, row = acc
            ps = name in BANKS
            for (j, lo2, hi2, row2, wr2) in seen.get(name, []):
                p = ops[j]
                if ps and p["q"] != o["q"]:
                    hit = True
                elif ps and o["q"] == "p":
                    hit = False
                else:
                    hit = (wr or wr2) and lo < hi2 and lo2 < hi and (row is None or row2 is None or row == row2)
                if hit and need.get(p["key"], (0, 0))[0] < p["n"]:
                    need[p["key"]] = (p["n"], j)
        for acc, wr in [(x, False) for x in o["r"]] + [(x, True) for x in o["w"]]:
            seen.setdefault(acc[0], []).append((i, acc[1], acc[2], acc[3], wr))
        if o["k"] == "x":
            o["clock"] = {}
            continue
        ck = clock[o["q"]]
        for key2, (n, j) in sorted(need.items(), key=lambda kv: -kv[1][1]):
            if ck.get(key2, 0) >= n:
                continue
            o["waits"].append(j)
            ops[j]["sig"] = True
            ck[key2] = n
            for k3, n3 in ops[j]["clock"].items():
                if ck.get(k3, 0) < n3:
                    ck[k3] = n3
        o["clock"] = dict(ck)
    val = {}
    nd = 0
    open_dmas = []
    for o in ops:
        if o["k"] == "d":
            o["sem"] = ("dm%d" % nd, 16)
            nd += 1
            if not o["sig"]:
                open_dmas.append(o)
        elif o["k"] == "c" and o["sig"]:
            val[o["q"]] = val.get(o["q"], 0) + 1
            o["sem"] = ("q" + o["q"], val[o["q"]])
    for o in ops:
        if o["k"] == "x":
            continue
        q = Q[o["q"]]
        for j in o["waits"]:
            q.wait_ge(T.sem[ops[j]["sem"][0]], ops[j]["sem"][1])
        ins = o["fn"]()
        if o["k"] == "d":
            ins.then_inc(T.sem[o["sem"][0]], 16)
        elif o["k"] == "c" and o["sig"]:
            ins.then_inc(T.sem[o["sem"][0]], 1)
    Q["g"].wait_ge(T.sem.sent, nsent)
    for o in open_dmas:
        Q["s"].wait_ge(T.sem[o["sem"][0]], 16)
